import numpy as np
import ml_dtypes


def mxq(x, axis, fmt="e4m3"):
    dtype, down = {"e4m3": (ml_dtypes.float8_e4m3fn, 7), "e5m2": (ml_dtypes.float8_e5m2, 14)}[fmt]
    v = np.moveaxis(np.asarray(x, np.float32).astype(ml_dtypes.bfloat16).astype(np.float64), axis, -1)
    blocks = v.reshape(v.shape[:-1] + (-1, 32))
    amax = np.abs(blocks).max(-1, keepdims=True)
    byte = np.maximum(np.where(amax > 0, np.frexp(amax)[1] - 1 + 127, 0) - down, 1)
    scale = np.exp2(byte - 127.0)
    codes = (blocks / scale).astype(np.float32).astype(dtype).astype(np.float64)
    return np.moveaxis((codes * scale).reshape(v.shape), -1, axis)


WIDE = False


def mx_kscale(k):
    if not WIDE:
        return np.ones(k)
    levels = np.array([10, -10, 5, -5, 0])
    if k % 512:
        return np.exp2(np.random.permutation(np.resize(levels, k // 32))).repeat(32)
    a = np.empty((k // 512, 16))
    for p in range(k // 512):
        a[p, :8] = np.random.permutation(np.resize(levels, 8))
        for g in range(8):
            far = levels[np.abs(levels - a[p, g]) >= 10]
            a[p, g + 8] = far[np.random.randint(len(far))]
    return np.exp2(a.ravel()).repeat(32)


def f64(x):
    return np.asarray(x).astype(np.float64)


def striped(idx):
    return np.tile(idx.reshape(-1, 16).T, (8, 1)).astype(np.uint16)


def unstriped(offs):
    return offs[:16].T.reshape(-1).astype(np.int64)


E2M1 = np.array([0.0, 0.5, 1.0, 1.5, 2.0, 3.0, 4.0, 6.0, -0.0, -0.5, -1.0, -1.5, -2.0, -3.0, -4.0, -6.0])


def pack_weight(w, fmt):
    k, n = w.shape
    w = f64(np.asarray(w, np.float32).astype(ml_dtypes.bfloat16)).reshape(k // 32, 32, n)
    amax = np.abs(w).max(1)
    if fmt == "e4m3":
        byte = np.frexp(amax)[1] - 1 + 127 - 7
    else:
        mant, ex = np.frexp(amax / 6.0)
        byte = np.where(mant > 0.5, ex, ex - 1) + 127
    byte = np.clip(np.where(amax > 0, byte, 1), 1, 254)
    scaled = (w * np.exp2(127.0 - byte)[:, None, :]).reshape(k, n).astype(np.float32)
    by_word = np.ascontiguousarray(scaled.reshape(k // 512, 128, 4, n).transpose(0, 1, 3, 2))
    if fmt == "e4m3":
        words = by_word.astype(ml_dtypes.float8_e4m3fn).view(np.uint8)
    else:
        c = by_word.astype(ml_dtypes.float4_e2m1fn).view(np.uint8) & 0xF
        words = (c[..., 0::2] | (c[..., 1::2] << 4)).reshape(k // 512, 128, 2 * n)
    return np.ascontiguousarray(words), np.ascontiguousarray(byte.astype(np.uint8).reshape(k // 512, 16, n))


def unpack_weight(words, scales, fmt):
    g, _, n = scales.shape
    words = np.ascontiguousarray(words).reshape(g, 128, n, -1)
    if fmt == "e4m3":
        vals = words.view(ml_dtypes.float8_e4m3fn).astype(np.float64)
    else:
        nib = np.empty((g, 128, n, 4), np.uint8)
        nib[..., 0::2] = words & 0xF
        nib[..., 1::2] = words >> 4
        vals = E2M1[nib]
    vals = vals * np.repeat(np.exp2(scales.astype(np.float64) - 127.0), 8, axis=1)[..., None]
    return vals.transpose(0, 1, 3, 2).reshape(g * 512, n)


def relu(v):
    return np.maximum(v, 0.0)


K, T, E, C, N = 1536, 512, 4, 256, 512
M = 384


def by_expert(wq, xq):
    return np.concatenate([wq[e].T @ xq[:, e * C:(e + 1) * C] for e in range(E)], axis=1)


def setup_inputs():
    n = np.random.standard_normal
    s = mx_kscale(K)[:, None]
    v = mx_kscale(N)
    first = np.random.permutation(np.repeat(np.arange(E), T // E))
    second = (first + 1 + np.random.permutation(np.repeat(np.arange(E - 1), -(-T // (E - 1)))[:T])) % E
    while np.bincount(second, minlength=E).max() != T // E:
        load = np.bincount(second, minlength=E); hi, lo = int(load.argmax()), int(load.argmin())
        t = np.flatnonzero((second == hi) & (first != lo))[0]; second[t] = lo
    slot_token = np.empty(E * C, np.int64); pos = np.empty((2, T), np.int64); fill = np.zeros(E, np.int64)
    place = np.stack([np.random.permutation(C) for _ in range(E)])
    for r, deal in enumerate((first, second)):
        for t in np.random.permutation(T):
            e = deal[t]; j = e * C + place[e, fill[e]]; fill[e] += 1; slot_token[j] = t; pos[r, t] = j
    g = np.random.uniform(0.2, 0.8, T)
    w = [pack_weight(m, "e2m1") for m in n((E, K, N)) / np.sqrt(K) / s[None] * v[None, None, :]]
    x = pack_weight(n((K, T)) * s, "e4m3")
    return {
        "x_words": x[0],
        "x_scales": x[1],
        "w_words": np.stack([m[0] for m in w]),
        "w_scales": np.stack([m[1] for m in w]),
        "b": (0.3 * n((N, E)) * v[:, None]).astype(np.float32),
        "wp": (n((N, M)) / np.sqrt(N) / v[:, None]).astype(np.float32),
        "gate": np.stack([np.tile(g, (N, 1)), np.tile(1.0 - g, (N, 1))]).astype(np.float32),
        "offs": striped(slot_token),
        "pos1": striped(pos[0]),
        "pos2": striped(pos[1]),
    }


def reference(x_words, x_scales, w_words, w_scales, b, wp, gate, offs, pos1, pos2):
    idx = unstriped(offs)
    w = np.stack([unpack_weight(w_words[e], w_scales[e], "e2m1") for e in range(E)])
    xq = unpack_weight(x_words, x_scales, "e4m3")[:, idx]
    y = by_expert(w, xq)
    y = relu(y + np.repeat(f64(b), C, axis=1))
    c = f64(gate[0]) * y[:, unstriped(pos1)] + f64(gate[1]) * y[:, unstriped(pos2)]
    return mxq(f64(wp), 0, "e4m3").T @ mxq(c, 0, "e4m3")

from contextlib import ExitStack

import concourse.mybir as mybir
from concourse.masks import make_identity

K, T, E, C, N, M = 1536, 512, 4, 256, 512, 384
S = E * C
P = 128
PASSES = K // 512
NB = N // P
TB = T // P
MB = M // P
FLOPS = 2 * K * N * S + 2 * N * M * T

F32 = mybir.dt.float32
BF16 = mybir.dt.bfloat16
I32 = mybir.dt.int32
U32 = mybir.dt.uint32
U16 = mybir.dt.uint16
U8 = mybir.dt.uint8
FP8X4 = mybir.dt.float8_e4m3fn_x4
FP4X4 = mybir.dt.float4_e2m1fn_x4
MULT = mybir.AluOpType.mult
RELU = mybir.ActivationFunctionType.Relu


def tile_moe_nxt_lin_relu_kernel(
    tc, x_words, x_scales, w_words, w_scales, b, wp, gate, offs, pos1, pos2, out
):
    nc = tc.nc
    with ExitStack() as ctx:
        keep = ctx.enter_context(tc.tile_pool(name="keep", bufs=1))
        ps_y = ctx.enter_context(tc.psum_pool(name="ps_y", bufs=3))
        ps_c = ctx.enter_context(tc.psum_pool(name="ps_c", bufs=2))
        ps_w = ctx.enter_context(tc.psum_pool(name="ps_w", bufs=1))
        ps_o = ctx.enter_context(tc.psum_pool(name="ps_o", bufs=2))

        offs_sb = keep.tile([P, S // 16], U16, name="offs_sb")
        pos_sb = [keep.tile([P, T // 16], U16, name=f"pos_sb{s}") for s in range(2)]
        xs_rows = keep.tile([P, T], U8, name="xs_rows", align_bytes=64)
        xw = keep.tile([P, PASSES, T], I32, name="xw", tag="then_wp", align_bytes=64)
        ww = keep.tile([P, E * PASSES, 2 * N], U8, name="ww", align_bytes=64)
        ws = keep.tile([P, E * PASSES, N], U8, name="ws", align_bytes=64)
        xs_slots = keep.tile([P, S], U8, name="xs_slots", tag="then_gates", align_bytes=64)
        xs_plane = [keep.tile([P, S], U8, name=f"xs_plane{a}", align_bytes=64) for a in range(PASSES)]
        xg = [keep.tile([P, S], U32, name=f"xg{a}", align_bytes=64) for a in range(PASSES)]
        bias = keep.tile([P, NB, E], F32, name="bias")
        ident = keep.tile([P, P], F32, name="ident")

        nc.gpsimd.memset(xs_rows[0:96, :].bitcast(I32), 0)
        warm = keep.tile([P, 1], F32, name="warm")
        nc.vector.memset(warm[:], 0.0)
        warm_out = keep.tile([P, 1], F32, name="warm_out")
        nc.vector.memset(ws[:].bitcast(I32), 0)
        for a in range(PASSES):
            nc.gpsimd.memset(xs_plane[a][:].bitcast(I32), 0)
        make_identity(nc, ident[:])

        nc.sync.dma_start(offs_sb[:], offs)
        xs_flat = x_scales.rearrange("a q t -> (a q) t").bitcast(I32)
        nc.sync.dma_start(out=xs_rows[96:128, :].bitcast(I32), in_=xs_flat[0:32, :])
        nc.sync.dma_start(pos_sb[0][:], pos1)
        nc.sync.dma_start(pos_sb[1][:], pos2)
        nc.sync.dma_start(out=xs_rows[0:16, :].bitcast(I32), in_=xs_flat[32:48, :])
        nc.scalar.activation(warm_out[:], warm[:], RELU)
        nc.sync.dma_start(out=xw[:], in_=x_words.rearrange("a p t r -> p a (t r)").bitcast(I32))
        ws_rows = w_scales.rearrange("e a q n -> q (e a) n").bitcast(I32)
        for quad in range(4):
            nc.scalar.dma_start(out=ws[32 * quad : 32 * quad + 4, :, :].bitcast(I32), in_=ws_rows[4 * quad : 4 * quad + 4, :, :])
        nc.sync.dma_start(out=ww[:].bitcast(I32), in_=w_words.rearrange("e a p n -> p (e a) n").bitcast(I32))
        nc.sync.dma_start(out=bias[:], in_=b.rearrange("(j p) e -> p j e", p=P))

        cols = C // 16
        for e in range(E):
            nc.vector.tensor_copy(xs_slots[:, e * C : (e + 1) * C], xs_rows[:].indirect(offs_sb[:, e * cols : (e + 1) * cols]))
        for a in range(PASSES):
            for quad in range(4):
                row = (96 + 16 * a) % P + 4 * quad
                queue = nc.sync if quad % 2 == 0 else nc.scalar
                queue.dma_start(out=xs_plane[a][32 * quad : 32 * quad + 4, :].bitcast(I32), in_=xs_slots[row : row + 4, :].bitcast(I32))
        cuts = [(e * C, (e + 1) * C) for e in range(E - 1)] + [(S - C, S - P), (S - P, S)]
        for lo, hi in cuts:
            for a in range(PASSES):
                nc.vector.tensor_copy(xg[a][:, lo:hi], xw[:, a, :].bitcast(U32).indirect(offs_sb[:, lo // 16 : hi // 16]))

        gates = keep.tile([P, 2, T], F32, name="gates", tag="then_gates", align_bytes=64)
        wp_raw = keep.tile([P, 4, M], F32, name="wp_raw", tag="then_wp", align_bytes=64)
        nc.sync.dma_start(out=gates[:], in_=gate[:, 0:P, :].rearrange("s p t -> p s t"))
        nc.sync.dma_start(out=wp_raw[:], in_=wp.rearrange("(p r) f -> p r f", r=4))

        y = [keep.tile([P, S], F32, name=f"y{j}") for j in range(NB)]
        for j, e in sorted(((j, e) for j in range(NB) for e in range(E)), key=lambda je: (je[0] + je[1], je[0])):
            if True:
                acc = ps_y.tile([P, C], F32, name="acc")
                for h in range(C // P):
                    slots = slice(e * C + h * P, e * C + (h + 1) * P)
                    for a in range(PASSES):
                        ea = e * PASSES + a
                        nc.tensor.matmul_mx(
                            out=acc[:, h * P : (h + 1) * P],
                            lhsT=ww[:, ea, 2 * j * P : 2 * (j + 1) * P].bitcast(FP4X4),
                            lhsT_scale=ws[:, ea, j * P : (j + 1) * P],
                            rhs=xg[a][:, slots].bitcast(FP8X4),
                            rhs_scale=xs_plane[a][:, slots],
                            start=(a == 0),
                            stop=(a == PASSES - 1),
                        )
                nc.scalar.activation(y[j][:, e * C : (e + 1) * C], acc[:], RELU, bias=bias[:, j, e : e + 1])

        c_rows = [keep.tile([P, 2, P, 2], BF16, name=f"c_rows{tb}", align_bytes=64) for tb in range(TB)]

        def gather(j, lo, hi):
            prods = []
            for s in range(2):
                prod = keep.tile([P, hi - lo], F32, name=f"prod{j}_{lo}_{s}", tag=f"prod{j}_{lo}_{s}", align_bytes=64)
                nc.vector.tensor_tensor(prod[:], y[j][:].indirect(pos_sb[s][:, lo // 16 : hi // 16]), gates[:, s, lo:hi], MULT)
                prods.append(prod)
            return prods

        def turn(j, prods, lo, hi):
            bank = ps_c.tile([P, hi - lo], F32, name="c_bank")
            for t0 in range(0, hi - lo, P):
                for s in range(2):
                    nc.tensor.matmul(bank[:, t0 : t0 + P], prods[s][:, t0 : t0 + P], ident[:], start=(s == 0), stop=(s == 1), is_transpose=True)
            for t0 in range(0, hi - lo, P):
                tb = (lo + t0) // P
                nc.scalar.copy(
                    out=c_rows[tb][:, :, 32 * j : 32 * (j + 1), :],
                    in_=bank[:, t0 : t0 + P].rearrange("t (i u v) -> t u i v", u=2, v=2),
                )

        def project(tb):
            words = c_rows[tb][:].rearrange("t u p v -> t (u p v)").bitcast(F32)
            turned = ps_w.tile([P, 2, P], F32, name="turned")
            for u in range(2):
                nc.tensor.transpose(turned[:, u, :], words[:, u * P : (u + 1) * P], ident[:])
            c_bf = keep.tile([P, P * 4], BF16, name=f"c_bf{tb}", align_bytes=64)
            nc.scalar.copy(out=c_bf[:].bitcast(F32).rearrange("p (t u) -> p t u", u=2), in_=turned[:].rearrange("p u t -> p t u"))
            c_codes = keep.tile([P, P], U32, name=f"c_codes{tb}", align_bytes=64)
            c_plane = keep.tile([P, P], U8, name=f"c_plane{tb}", align_bytes=64)
            nc.vector.quantize_mx(out=c_codes[:].bitcast(FP8X4), scales=c_plane[:], in_=c_bf[:])
            res = ps_o.tile([P, MB, P], F32, name="res")
            for m in range(MB):
                nc.tensor.matmul_mx(
                    out=res[:, m, :],
                    lhsT=wp_codes[:, m * P : (m + 1) * P].bitcast(FP8X4),
                    lhsT_scale=wp_plane[:, m * P : (m + 1) * P],
                    rhs=c_codes[:].bitcast(FP8X4),
                    rhs_scale=c_plane[:],
                    start=True,
                    stop=True,
                )
            res_sb = keep.tile([P, MB, P], F32, name=f"res_sb{tb}")
            nc.vector.tensor_copy(out=res_sb[:], in_=res[:])
            nc.sync.dma_start(out=out[:, tb * P : (tb + 1) * P].rearrange("(m p) t -> p m t", p=P), in_=res_sb[:])

        for j in range(NB - 1):
            turn(j, gather(j, 0, T), 0, T)
        wp_bf = keep.tile([P, M, 4], BF16, name="wp_bf", tag="prod0_0_0", align_bytes=64)
        wp_codes = keep.tile([P, M], U32, name="wp_codes", align_bytes=64)
        wp_plane = keep.tile([P, M], U8, name="wp_plane", align_bytes=64)
        nc.scalar.copy(out=wp_bf[:], in_=wp_raw[:].rearrange("p r f -> p f r"))
        for lo, hi in ((0, 256), (256, M)):
            nc.vector.quantize_mx(out=wp_codes[:, lo:hi].bitcast(FP8X4), scales=wp_plane[:, lo:hi], in_=wp_bf[:, lo:hi, :].rearrange("p f r -> p (f r)"))
        last = [gather(NB - 1, tb * P, (tb + 1) * P) for tb in range(TB)]
        for tb in range(TB):
            turn(NB - 1, last[tb], tb * P, (tb + 1) * P)
            project(tb)
